import numpy as np
CORES = [1,129,9,137,57,185,105,233,113,241,121,249]
N = 12
TK = 512
D = 128 * N
EPS = 0.01
def setup_inputs(rng):
    return {"x": (rng.standard_normal((N, 128, TK), dtype=np.float32) * (0.5 + np.abs(rng.standard_normal((1, 1, TK), dtype=np.float32))) + rng.standard_normal((1, 1, TK), dtype=np.float32)), "w": (rng.standard_normal((N, 128, 128), dtype=np.float32) / 11)}
def reference(x, w):
    X = x.astype(np.float64)
    mu = X.sum(axis=(0, 1)) / D
    Z = X - mu
    Z = Z / np.sqrt((Z ** 2).sum(axis=(0, 1)) / D + EPS)
    s = sum(w[r].astype(np.float64).T @ Z[r] for r in range(N)).astype(np.float32)
    return {"y": np.broadcast_to(s, (N,) + s.shape)}

@@ -1,0 +1,257 @@
+from concourse.bass import DstId, RemoteDMATransfer
+from concourse.mybir import AluOpType, ActivationFunctionType
+
+N = 12
+TK = 512
+BL = 128
+S = TK // BL
+G = N // S
+D = 128 * N
+EPS = 0.01
+PW = 131
+PS = 132
+NSIM = 256
+
+SCRATCH = {
+    "xs": ("sbuf", [128, TK], "float32"),
+    "xq": ("sbuf", [128, TK], "float32"),
+    "wa": ("sbuf", [128, PS], "float32"),
+    "pay": ("sbuf", [128, S * PS], "float32"),
+    "yl": ("sbuf", [128, TK], "float32"),
+    "l1": ("sbuf", [128, S * PS], "float32"),
+    "l2": ("sbuf", [128, 2 * PS], "float32"),
+    "pa": ("sbuf", [128, PS], "float32"),
+    "pb": ("sbuf", [128, PS], "float32"),
+    "part": ("sbuf", [128, PS], "float32"),
+    "ones": ("sbuf", [128, 128], "float32"),
+    "idn": ("sbuf", [128, 128], "float32"),
+    "sta": ("sbuf", [128, 4], "float32"),
+    "st": ("sbuf", [128, 4], "float32"),
+    "col": ("sbuf", [128, 8], "float32"),
+    "dcw": ("sbuf", [128, 128], "float32"),
+    "pt": ("sbuf", [128, 128], "float32"),
+    "pt2": ("sbuf", [128, 128], "float32"),
+    "tmp": ("sbuf", [128, 128], "float32"),
+    "am": ("sbuf", [128, 128], "float32"),
+    "dg": ("sbuf", [128, 128], "float32"),
+    "yo": ("sbuf", [128, 128], "float32"),
+    "ps0": ("psum", [128, 512], "float32"),
+    "ps1": ("psum", [128, 512], "float32"),
+    "ps2": ("psum", [128, 512], "float32"),
+    "ps3": ("psum", [128, 512], "float32"),
+    "psc": ("psum", [128, 512], "float32"),
+}
+SEMAPHORES = (["ldw", "ms", "pec", "cwc", "lsem", "p3", "st", "idn", "p2_0", "p2_1"]
+              + ["ldx%d" % j for j in range(S)] + ["sq%d" % j for j in range(S)] + ["pe%d" % j for j in range(S)]
+              + ["ev%d" % j for j in range(S)] + ["p1_%d" % j for j in range(S)] + ["e%d" % k for k in range(20)])
+
+
+def _bits(mask):
+    return [e for e in range(mask.bit_length()) if (mask >> e) & 1]
+
+
+def _mask(bits):
+    m = 0
+    for e in bits:
+        m |= 1 << e
+    return m
+
+
+def _plan(T, topo):
+    cores = list(T.cores)
+    planes = []
+    for c in cores:
+        home = [p for p in planes if topo.same_plane(c, p[0])]
+        if home:
+            home[0].append(c)
+        else:
+            planes.append([c])
+    planes.sort(key=len)
+    small, big = planes
+    near = [[b for b in big if topo.mates(b, e)][0] for e in small]
+    far = [b for b in big if b not in near]
+    red = {}
+    for c in cores:
+        red[c] = [k for k in range(NSIM)
+                  if topo.host(k) == topo.host(c) and topo.chip(k) == topo.chip(c) and topo.die(k) == topo.die(c)
+                  and k not in cores and all(topo.may_write(k, d) for d in cores)][0]
+    return [small, near, far], red
+
+
+def _engines(topo, src, near_dst, far_dst):
+    off = _bits(topo.mask(src, far_dst))
+    spare = [e for e in _bits(topo.mask(src, near_dst)) if e not in off]
+    return off, spare
+
+
+def _step3(topo, grp, red, s):
+    src = red[grp[s]]
+    others = [grp[(s + k) % S] for k in range(1, S)]
+    off, spare = _engines(topo, src, grp[s], others[0])
+    h = len(off) // 2
+    return [[(others[0], off[:h]), (others[1], off[h:])], [(others[2], off)], [(grp[s], spare)]]
+
+
+def _rank(g, core, T, topo, groups, red):
+    sem = T.sem
+    grp = [q for q in groups if core in q][0]
+    i = grp.index(core)
+    order = [(i + 1 + j) % S for j in range(S)]
+    blk = [slice(b * BL, (b + 1) * BL) for b in order]
+
+    g.scalar.dma_start(T.wa[:, 0:128], T.w[:, :]).then_inc(sem.ldw, 16)
+    for j in range(S):
+        q = g.sync if j % 2 == 0 else g.scalar
+        q.dma_start(T.xs[:, blk[j]], T.x[:, blk[j]]).then_inc(sem["ldx%d" % j], 16)
+    g.vector.memset(T.wa[:, 128:PS], 1.0).then_inc(sem.ms, 1)
+
+    for j in range(S):
+        g.scalar.wait_ge(sem["ldx%d" % j], 16)
+        g.scalar.activation(T.xq[:, blk[j]], T.xs[:, blk[j]], ActivationFunctionType.Square).then_inc(sem["sq%d" % j], 1)
+
+    g.tensor.wait_ge(sem.ldw, 16)
+    g.tensor.wait_ge(sem.ms, 1)
+    for j in range(S):
+        ps = T["ps%d" % j]
+        g.tensor.wait_ge(sem["ldx%d" % j], 16)
+        g.tensor.matmul(ps[:, 0:129], T.xs[:, blk[j]], T.wa[:, 0:129], True, True).then_inc(sem["pe%d" % j], 1)
+        if j == 0:
+            g.tensor.matmul(T.psc[:, 0:1], T.wa[:, 0:128], T.wa[:, 128:129], True, True).then_inc(sem.pec, 1)
+        g.tensor.wait_ge(sem["sq%d" % j], 1)
+        g.tensor.matmul(ps[:, 129:130], T.xq[:, blk[j]], T.wa[:, 128:129], True, True).then_inc(sem["pe%d" % j], 1)
+
+    g.vector.wait_ge(sem.pec, 1)
+    for j in range(S):
+        g.vector.tensor_copy(T.pay[:, j * PS + 130:j * PS + 131], T.psc[:, 0:1]).then_inc(sem.cwc, 1)
+    for j in range(S):
+        g.vector.wait_ge(sem["pe%d" % j], 2)
+        g.vector.tensor_copy(T.pay[:, j * PS:j * PS + 130], T["ps%d" % j][:, 0:130]).then_inc(sem["ev%d" % j], 1)
+
+    off, spare = _engines(topo, core, red[core], red[grp[order[0]]])
+    sent = 0
+    g.wait_ge(sem.cwc, S)
+    for j in range(S):
+        dst = red[grp[order[j]]]
+        eng = spare if dst == red[core] else off
+        rid, pid = topo.addr(dst, core)
+        g.wait_ge(sem["ev%d" % j], 1)
+        g.remote_dma(out_ap=T.l1[:, j * PS:j * PS + PW], in_ap=T.pay[:, j * PS:j * PS + PW],
+                     remote_sem=sem["p1_%d" % j], local_sem=sem.lsem, pid=pid, routing_id=rid,
+                     dma_engine_mask=_mask(eng))
+        sent += len(eng)
+
+    due = 0
+    for s in range(S):
+        for call in _step3(topo, grp, red, s):
+            due += sum(len(eng) for dst, eng in call if dst == core)
+    g.sync.wait_ge(sem.p3, due)
+    g.sync.dma_start(T.y[:, :], T.yl[:, :]).then_inc(sem.st, 16)
+    g.sync.wait_ge(sem.st, 16)
+    g.wait_ge(sem.lsem, sent)
+
+
+def _reducer(g, core, T, topo, groups, red):
+    sem = T.sem
+    owner = [c for c in red if red[c] == core][0]
+    gi = [k for k in range(G) if owner in groups[k]][0]
+    grp = groups[gi]
+    s = grp.index(owner)
+    V, add, mult = g.vector, AluOpType.add, AluOpType.mult
+    nev = [0]
+
+    def ev():
+        nev[0] += 1
+        return sem["e%d" % (nev[0] - 1)]
+
+    V.memset(T.ones[:, :], 1.0).then_inc(sem.ms, 1)
+    g.wait_ge(sem.ms, 1)
+    g.affine_select(T.idn[:, :], T.ones[:, :], [[-1, 128]], AluOpType.is_equal, 0.0, 0, 1).then_inc(sem.idn, 1)
+
+    off, spare = _engines(topo, core, owner, red[grp[(s + 1) % S]])
+    cnt = [len(off)] * (S - 1) + [len(spare)]
+    L = [T.l1[:, j * PS:j * PS + PW] for j in range(S)]
+    e_a, e_b, e_part = ev(), ev(), ev()
+    V.wait_ge(sem.p1_0, cnt[0])
+    V.wait_ge(sem.p1_1, cnt[1])
+    V.tensor_tensor(T.pa[:, 0:PW], L[0], L[1], add).then_inc(e_a, 1)
+    V.wait_ge(sem.p1_2, cnt[2])
+    V.wait_ge(e_a, 1)
+    V.tensor_tensor(T.pb[:, 0:PW], T.pa[:, 0:PW], L[2], add).then_inc(e_b, 1)
+    V.wait_ge(sem.p1_3, cnt[3])
+    V.wait_ge(e_b, 1)
+    V.tensor_tensor(T.part[:, 0:PW], T.pb[:, 0:PW], L[3], add).then_inc(e_part, 1)
+
+    h = len(off) // 2
+    trs = []
+    for k in range(1, G):
+        go = (gi + k) % G
+        dst = red[groups[go][s]]
+        slot = (gi - go - 1) % G
+        rid, pid = topo.addr(dst, core)
+        trs.append(RemoteDMATransfer(dst_ids=[DstId(rid=rid, pnc=pid)], dma_engine_mask=_mask(off[(k - 1) * h:k * h]),
+                                     remote_sem=sem["p2_%d" % slot], src=T.part[:, 0:PW],
+                                     dst=T.l2[:, slot * PS:slot * PS + PW]))
+    g.wait_ge(e_part, 1)
+    g.remote_dma_fused(trs, local_sem=sem.lsem)
+    sent = 2 * h
+
+    A0, A1 = T.l2[:, 0:PS], T.l2[:, PS:2 * PS]
+    s1, s2, cw = T.st[:, 0:1], T.st[:, 1:2], T.st[:, 2:3]
+    c_a, c_c, c_sd, c_nmu, c_r = (T.col[:, k:k + 1] for k in range(5))
+    e1, e2, e3, e4, e5, e6, e7, e8 = (ev() for _ in range(8))
+    V.wait_ge(e_part, 1)
+    V.wait_ge(sem.p2_0, h)
+    V.tensor_tensor(T.sta[:, 0:3], T.part[:, 128:PW], A0[:, 128:PW], add).then_inc(e1, 1)
+    V.wait_ge(sem.p2_1, h)
+    V.wait_ge(e1, 1)
+    V.tensor_tensor(T.st[:, 0:3], T.sta[:, 0:3], A1[:, 128:PW], add).then_inc(e2, 1)
+    V.wait_ge(e2, 1)
+    V.tensor_scalar(c_a, s1, s1, -1.0 / D, mult, mult).then_inc(e3, 1)
+    V.wait_ge(e3, 1)
+    V.tensor_tensor(c_c, c_a, s2, add).then_inc(e4, 1)
+    g.scalar.wait_ge(e4, 1)
+    g.scalar.activation(c_sd, c_c, ActivationFunctionType.Sqrt, bias=EPS, scale=1.0 / D).then_inc(e5, 1)
+    V.wait_ge(sem.idn, 1)
+    V.tensor_scalar(T.dcw[:, :], T.idn[:, :], cw, None, mult).then_inc(e6, 1)
+    g.tensor.wait_ge(sem.ms, 1)
+    g.tensor.wait_ge(e6, 1)
+    g.tensor.matmul(T.ps0[:, 0:128], T.ones[:, :], T.dcw[:, :], True, True).then_inc(e7, 1)
+    V.tensor_scalar(c_nmu, s1, -1.0 / D, None, mult).then_inc(e8, 1)
+    e9, e10, e11, e12, e13, e14, e15, e16 = (ev() for _ in range(8))
+    V.tensor_tensor(T.pt[:, :], T.part[:, 0:128], A0[:, 0:128], add).then_inc(e9, 1)
+    V.wait_ge(e9, 1)
+    V.tensor_tensor(T.pt2[:, :], T.pt[:, :], A1[:, 0:128], add).then_inc(e10, 1)
+    V.wait_ge(e7, 1)
+    V.wait_ge(e8, 1)
+    V.tensor_scalar(T.tmp[:, :], T.ps0[:, 0:128], c_nmu, None, mult).then_inc(e11, 1)
+    V.wait_ge(e10, 1)
+    V.wait_ge(e11, 1)
+    V.tensor_tensor(T.am[:, :], T.tmp[:, :], T.pt2[:, :], add).then_inc(e12, 1)
+    V.wait_ge(e5, 1)
+    V.reciprocal(c_r, c_sd).then_inc(e13, 1)
+    V.wait_ge(e13, 1)
+    V.tensor_scalar(T.dg[:, :], T.idn[:, :], c_r, None, mult).then_inc(e14, 1)
+    g.tensor.wait_ge(e12, 1)
+    g.tensor.wait_ge(e14, 1)
+    g.tensor.matmul(T.ps1[:, 0:128], T.am[:, :], T.dg[:, :], True, True).then_inc(e15, 1)
+    V.wait_ge(e15, 1)
+    V.tensor_copy(T.yo[:, :], T.ps1[:, 0:128]).then_inc(e16, 1)
+
+    g.wait_ge(e16, 1)
+    for call in _step3(topo, grp, red, s):
+        trs = []
+        for dst, eng in call:
+            rid, pid = topo.addr(dst, core)
+            trs.append(RemoteDMATransfer(dst_ids=[DstId(rid=rid, pnc=pid)], dma_engine_mask=_mask(eng), remote_sem=sem.p3,
+                                         src=T.yo[:, :], dst=T.yl[:, s * BL:(s + 1) * BL]))
+            sent += len(eng)
+        g.remote_dma_fused(trs, local_sem=sem.lsem)
+    g.wait_ge(sem.lsem, sent)
+
+
+def rank_program(g, core, T, topo):
+    groups, red = _plan(T, topo)
+    if T.rank_of(core) is not None:
+        _rank(g, core, T, topo, groups, red)
+    elif core in red.values():
+        _reducer(g, core, T, topo, groups, red)

@@ -19,9 +19,7 @@ SCRATCH = {
     "pay": ("sbuf", [128, S * PS], "float32"),
     "yl": ("sbuf", [128, TK], "float32"),
     "l1": ("sbuf", [128, S * PS], "float32"),
-    "l2": ("sbuf", [128, 2 * PS], "float32"),
-    "pa": ("sbuf", [128, PS], "float32"),
-    "pb": ("sbuf", [128, PS], "float32"),
+    "l2": ("sbuf", [128, 4 * PS], "float32"),
     "part": ("sbuf", [128, PS], "float32"),
     "ones": ("sbuf", [128, 128], "float32"),
     "idn": ("sbuf", [128, 128], "float32"),
@@ -29,8 +27,6 @@ SCRATCH = {
     "st": ("sbuf", [128, 4], "float32"),
     "col": ("sbuf", [128, 8], "float32"),
     "dcw": ("sbuf", [128, 128], "float32"),
-    "pt": ("sbuf", [128, 128], "float32"),
-    "pt2": ("sbuf", [128, 128], "float32"),
     "tmp": ("sbuf", [128, 128], "float32"),
     "am": ("sbuf", [128, 128], "float32"),
     "dg": ("sbuf", [128, 128], "float32"),
@@ -41,9 +37,10 @@ SCRATCH = {
     "ps3": ("psum", [128, 512], "float32"),
     "psc": ("psum", [128, 512], "float32"),
 }
-SEMAPHORES = (["ldw", "ms", "pec", "cwc", "lsem", "p3", "st", "idn", "p2_0", "p2_1"]
+SEMAPHORES = (["ldw", "ms", "pec", "cwc", "lsem", "st0", "st1", "idn", "p2a_0", "p2a_1", "p2b_0", "p2b_1"]
               + ["ldx%d" % j for j in range(S)] + ["sq%d" % j for j in range(S)] + ["pe%d" % j for j in range(S)]
-              + ["ev%d" % j for j in range(S)] + ["p1_%d" % j for j in range(S)] + ["e%d" % k for k in range(20)])
+              + ["ev%d" % j for j in range(S)] + ["p1_%d" % j for j in range(S)] + ["p3_%d" % j for j in range(S)]
+              + ["e%d" % k for k in range(24)])
 
 
 def _bits(mask):
@@ -140,13 +137,18 @@ def _rank(g, core, T, topo, groups, red):
                      dma_engine_mask=_mask(eng))
         sent += len(eng)
 
-    due = 0
+    when = []
     for s in range(S):
-        for call in _step3(topo, grp, red, s):
-            due += sum(len(eng) for dst, eng in call if dst == core)
-    g.sync.wait_ge(sem.p3, due)
-    g.sync.dma_start(T.y[:, :], T.yl[:, :]).then_inc(sem.st, 16)
-    g.sync.wait_ge(sem.st, 16)
+        for k, call in enumerate(_step3(topo, grp, red, s)):
+            when += [(k, s, len(eng)) for dst, eng in call if dst == core]
+    far = sorted(e for e in when if e[1] != i)
+    own = [e for e in when if e[1] == i]
+    plan = [(g.sync, sem.st0, [far[0], far[2]]), (g.scalar, sem.st1, [far[1], own[0]])]
+    for q, done, todo in plan:
+        for k, s, n in todo:
+            q.wait_ge(sem["p3_%d" % s], n)
+            q.dma_start(T.y[:, s * BL:(s + 1) * BL], T.yl[:, s * BL:(s + 1) * BL]).then_inc(done, 16)
+        q.wait_ge(done, 16 * len(todo))
     g.wait_ge(sem.lsem, sent)
 
 
@@ -170,39 +172,53 @@ def _reducer(g, core, T, topo, groups, red):
     off, spare = _engines(topo, core, owner, red[grp[(s + 1) % S]])
     cnt = [len(off)] * (S - 1) + [len(spare)]
     L = [T.l1[:, j * PS:j * PS + PW] for j in range(S)]
-    e_a, e_b, e_part = ev(), ev(), ev()
-    V.wait_ge(sem.p1_0, cnt[0])
-    V.wait_ge(sem.p1_1, cnt[1])
-    V.tensor_tensor(T.pa[:, 0:PW], L[0], L[1], add).then_inc(e_a, 1)
-    V.wait_ge(sem.p1_2, cnt[2])
-    V.wait_ge(e_a, 1)
-    V.tensor_tensor(T.pb[:, 0:PW], T.pa[:, 0:PW], L[2], add).then_inc(e_b, 1)
-    V.wait_ge(sem.p1_3, cnt[3])
-    V.wait_ge(e_b, 1)
-    V.tensor_tensor(T.part[:, 0:PW], T.pb[:, 0:PW], L[3], add).then_inc(e_part, 1)
-
     h = len(off) // 2
-    trs = []
-    for k in range(1, G):
-        go = (gi + k) % G
-        dst = red[groups[go][s]]
-        slot = (gi - go - 1) % G
-        rid, pid = topo.addr(dst, core)
-        trs.append(RemoteDMATransfer(dst_ids=[DstId(rid=rid, pnc=pid)], dma_engine_mask=_mask(off[(k - 1) * h:k * h]),
-                                     remote_sem=sem["p2_%d" % slot], src=T.part[:, 0:PW],
-                                     dst=T.l2[:, slot * PS:slot * PS + PW]))
-    g.wait_ge(e_part, 1)
-    g.remote_dma_fused(trs, local_sem=sem.lsem)
-    sent = 2 * h
 
-    A0, A1 = T.l2[:, 0:PS], T.l2[:, PS:2 * PS]
+    def step2(stage, src):
+        trs = []
+        for k in range(1, G):
+            go = (gi + k) % G
+            dst = red[groups[go][s]]
+            slot = (gi - go - 1) % G
+            rid, pid = topo.addr(dst, core)
+            at = (2 * stage + slot) * PS
+            trs.append(RemoteDMATransfer(dst_ids=[DstId(rid=rid, pnc=pid)], dma_engine_mask=_mask(off[(k - 1) * h:k * h]),
+                                         remote_sem=sem["p2%s_%d" % ("ab"[stage], slot)], src=src,
+                                         dst=T.l2[:, at:at + PW]))
+        g.remote_dma_fused(trs, local_sem=sem.lsem)
+
+    g.wait_ge(sem.p1_0, cnt[0])
+    step2(0, L[0])
+    pa, b0, b1, base = T.ps2[:, 0:PW], T.ps3[:, 0:PW], T.ps2[:, 256:256 + PW], T.ps3[:, 256:256 + PW]
+    e_a, e_part, e_b0, e_b1, e_base = (ev() for _ in range(5))
+    V.wait_ge(sem.p1_1, cnt[1])
+    V.wait_ge(sem.p1_2, cnt[2])
+    V.tensor_tensor(pa, L[1], L[2], add).then_inc(e_a, 1)
+    V.wait_ge(sem.p1_3, cnt[3])
+    V.wait_ge(e_a, 1)
+    V.tensor_tensor(T.part[:, 0:PW], pa, L[3], add).then_inc(e_part, 1)
+    g.wait_ge(e_part, 1)
+    step2(1, T.part[:, 0:PW])
+    sent = 4 * h
+    V.wait_ge(sem.p1_0, cnt[0])
+    V.wait_ge(e_part, 1)
+    V.tensor_tensor(b0, T.part[:, 0:PW], L[0], add).then_inc(e_b0, 1)
+    V.wait_ge(sem.p2a_0, h)
+    V.wait_ge(e_b0, 1)
+    V.tensor_tensor(b1, b0, T.l2[:, 0:PW], add).then_inc(e_b1, 1)
+    V.wait_ge(sem.p2a_1, h)
+    V.wait_ge(e_b1, 1)
+    V.tensor_tensor(base, b1, T.l2[:, PS:PS + PW], add).then_inc(e_base, 1)
+
+    A0, A1 = T.l2[:, 2 * PS:3 * PS], T.l2[:, 3 * PS:4 * PS]
     s1, s2, cw = T.st[:, 0:1], T.st[:, 1:2], T.st[:, 2:3]
+    pt, pt2 = T.psc[:, 0:128], T.psc[:, 128:256]
     c_a, c_c, c_sd, c_nmu, c_r = (T.col[:, k:k + 1] for k in range(5))
     e1, e2, e3, e4, e5, e6, e7, e8 = (ev() for _ in range(8))
-    V.wait_ge(e_part, 1)
-    V.wait_ge(sem.p2_0, h)
-    V.tensor_tensor(T.sta[:, 0:3], T.part[:, 128:PW], A0[:, 128:PW], add).then_inc(e1, 1)
-    V.wait_ge(sem.p2_1, h)
+    V.wait_ge(e_base, 1)
+    V.wait_ge(sem.p2b_0, h)
+    V.tensor_tensor(T.sta[:, 0:3], base[:, 128:PW], A0[:, 128:PW], add).then_inc(e1, 1)
+    V.wait_ge(sem.p2b_1, h)
     V.wait_ge(e1, 1)
     V.tensor_tensor(T.st[:, 0:3], T.sta[:, 0:3], A1[:, 128:PW], add).then_inc(e2, 1)
     V.wait_ge(e2, 1)
@@ -218,15 +234,15 @@ def _reducer(g, core, T, topo, groups, red):
     g.tensor.matmul(T.ps0[:, 0:128], T.ones[:, :], T.dcw[:, :], True, True).then_inc(e7, 1)
     V.tensor_scalar(c_nmu, s1, -1.0 / D, None, mult).then_inc(e8, 1)
     e9, e10, e11, e12, e13, e14, e15, e16 = (ev() for _ in range(8))
-    V.tensor_tensor(T.pt[:, :], T.part[:, 0:128], A0[:, 0:128], add).then_inc(e9, 1)
+    V.tensor_tensor(pt, base[:, 0:128], A0[:, 0:128], add).then_inc(e9, 1)
     V.wait_ge(e9, 1)
-    V.tensor_tensor(T.pt2[:, :], T.pt[:, :], A1[:, 0:128], add).then_inc(e10, 1)
+    V.tensor_tensor(pt2, pt, A1[:, 0:128], add).then_inc(e10, 1)
     V.wait_ge(e7, 1)
     V.wait_ge(e8, 1)
     V.tensor_scalar(T.tmp[:, :], T.ps0[:, 0:128], c_nmu, None, mult).then_inc(e11, 1)
     V.wait_ge(e10, 1)
     V.wait_ge(e11, 1)
-    V.tensor_tensor(T.am[:, :], T.tmp[:, :], T.pt2[:, :], add).then_inc(e12, 1)
+    V.tensor_tensor(T.am[:, :], T.tmp[:, :], pt2, add).then_inc(e12, 1)
     V.wait_ge(e5, 1)
     V.reciprocal(c_r, c_sd).then_inc(e13, 1)
     V.wait_ge(e13, 1)
@@ -242,8 +258,8 @@ def _reducer(g, core, T, topo, groups, red):
         trs = []
         for dst, eng in call:
             rid, pid = topo.addr(dst, core)
-            trs.append(RemoteDMATransfer(dst_ids=[DstId(rid=rid, pnc=pid)], dma_engine_mask=_mask(eng), remote_sem=sem.p3,
-                                         src=T.yo[:, :], dst=T.yl[:, s * BL:(s + 1) * BL]))
+            trs.append(RemoteDMATransfer(dst_ids=[DstId(rid=rid, pnc=pid)], dma_engine_mask=_mask(eng),
+                                         remote_sem=sem["p3_%d" % s], src=T.yo[:, :], dst=T.yl[:, s * BL:(s + 1) * BL]))
             sent += len(eng)
         g.remote_dma_fused(trs, local_sem=sem.lsem)
     g.wait_ge(sem.lsem, sent)

from concourse.bass import DstId, RemoteDMATransfer
from concourse.mybir import AluOpType, ActivationFunctionType

N = 12
TK = 512
BL = 128
S = TK // BL
G = N // S
D = 128 * N
EPS = 0.01
PW = 131
PS = 132
NSIM = 256

SCRATCH = {
    "xs": ("sbuf", [128, TK], "float32"),
    "xq": ("sbuf", [128, TK], "float32"),
    "wa": ("sbuf", [128, PS], "float32"),
    "pay": ("sbuf", [128, S * PS], "float32"),
    "yl": ("sbuf", [128, TK], "float32"),
    "l1": ("sbuf", [128, S * PS], "float32"),
    "l2": ("sbuf", [128, 4 * PS], "float32"),
    "part": ("sbuf", [128, PS], "float32"),
    "ones": ("sbuf", [128, 128], "float32"),
    "idn": ("sbuf", [128, 128], "float32"),
    "sta": ("sbuf", [128, 4], "float32"),
    "st": ("sbuf", [128, 4], "float32"),
    "col": ("sbuf", [128, 8], "float32"),
    "dcw": ("sbuf", [128, 128], "float32"),
    "tmp": ("sbuf", [128, 128], "float32"),
    "am": ("sbuf", [128, 128], "float32"),
    "dg": ("sbuf", [128, 128], "float32"),
    "yo": ("sbuf", [128, 128], "float32"),
    "ps0": ("psum", [128, 512], "float32"),
    "ps1": ("psum", [128, 512], "float32"),
    "ps2": ("psum", [128, 512], "float32"),
    "ps3": ("psum", [128, 512], "float32"),
    "psc": ("psum", [128, 512], "float32"),
}
SEMAPHORES = (["ldw", "ms", "pec", "cwc", "lsem", "st0", "st1", "idn", "p2a_0", "p2a_1", "p2b_0", "p2b_1"]
              + ["ldx%d" % j for j in range(S)] + ["sq%d" % j for j in range(S)] + ["pe%d" % j for j in range(S)]
              + ["ev%d" % j for j in range(S)] + ["p1_%d" % j for j in range(S)] + ["p3_%d" % j for j in range(S)]
              + ["e%d" % k for k in range(24)])


def _bits(mask):
    return [e for e in range(mask.bit_length()) if (mask >> e) & 1]


def _mask(bits):
    m = 0
    for e in bits:
        m |= 1 << e
    return m


def _plan(T, topo):
    cores = list(T.cores)
    planes = []
    for c in cores:
        home = [p for p in planes if topo.same_plane(c, p[0])]
        if home:
            home[0].append(c)
        else:
            planes.append([c])
    planes.sort(key=len)
    small, big = planes
    near = [[b for b in big if topo.mates(b, e)][0] for e in small]
    far = [b for b in big if b not in near]
    red = {}
    for c in cores:
        red[c] = [k for k in range(NSIM)
                  if topo.host(k) == topo.host(c) and topo.chip(k) == topo.chip(c) and topo.die(k) == topo.die(c)
                  and k not in cores and all(topo.may_write(k, d) for d in cores)][0]
    return [small, near, far], red


def _engines(topo, src, near_dst, far_dst):
    off = _bits(topo.mask(src, far_dst))
    spare = [e for e in _bits(topo.mask(src, near_dst)) if e not in off]
    return off, spare


def _step3(topo, grp, red, s):
    src = red[grp[s]]
    others = [grp[(s + k) % S] for k in range(1, S)]
    off, spare = _engines(topo, src, grp[s], others[0])
    h = len(off) // 2
    return [[(others[0], off[:h]), (others[1], off[h:])], [(others[2], off)], [(grp[s], spare)]]


def _rank(g, core, T, topo, groups, red):
    sem = T.sem
    grp = [q for q in groups if core in q][0]
    i = grp.index(core)
    order = [(i + 1 + j) % S for j in range(S)]
    blk = [slice(b * BL, (b + 1) * BL) for b in order]

    g.scalar.dma_start(T.wa[:, 0:128], T.w[:, :]).then_inc(sem.ldw, 16)
    for j in range(S):
        q = g.sync if j % 2 == 0 else g.scalar
        q.dma_start(T.xs[:, blk[j]], T.x[:, blk[j]]).then_inc(sem["ldx%d" % j], 16)
    g.vector.memset(T.wa[:, 128:PS], 1.0).then_inc(sem.ms, 1)

    for j in range(S):
        g.scalar.wait_ge(sem["ldx%d" % j], 16)
        g.scalar.activation(T.xq[:, blk[j]], T.xs[:, blk[j]], ActivationFunctionType.Square).then_inc(sem["sq%d" % j], 1)

    g.tensor.wait_ge(sem.ldw, 16)
    g.tensor.wait_ge(sem.ms, 1)
    for j in range(S):
        ps = T["ps%d" % j]
        g.tensor.wait_ge(sem["ldx%d" % j], 16)
        g.tensor.matmul(ps[:, 0:129], T.xs[:, blk[j]], T.wa[:, 0:129], True, True).then_inc(sem["pe%d" % j], 1)
        if j == 0:
            g.tensor.matmul(T.psc[:, 0:1], T.wa[:, 0:128], T.wa[:, 128:129], True, True).then_inc(sem.pec, 1)
        g.tensor.wait_ge(sem["sq%d" % j], 1)
        g.tensor.matmul(ps[:, 129:130], T.xq[:, blk[j]], T.wa[:, 128:129], True, True).then_inc(sem["pe%d" % j], 1)

    g.vector.wait_ge(sem.pec, 1)
    for j in range(S):
        g.vector.tensor_copy(T.pay[:, j * PS + 130:j * PS + 131], T.psc[:, 0:1]).then_inc(sem.cwc, 1)
    for j in range(S):
        g.vector.wait_ge(sem["pe%d" % j], 2)
        g.vector.tensor_copy(T.pay[:, j * PS:j * PS + 130], T["ps%d" % j][:, 0:130]).then_inc(sem["ev%d" % j], 1)

    off, spare = _engines(topo, core, red[core], red[grp[order[0]]])
    sent = 0
    g.wait_ge(sem.cwc, S)
    for j in range(S):
        dst = red[grp[order[j]]]
        eng = spare if dst == red[core] else off
        rid, pid = topo.addr(dst, core)
        g.wait_ge(sem["ev%d" % j], 1)
        g.remote_dma(out_ap=T.l1[:, j * PS:j * PS + PW], in_ap=T.pay[:, j * PS:j * PS + PW],
                     remote_sem=sem["p1_%d" % j], local_sem=sem.lsem, pid=pid, routing_id=rid,
                     dma_engine_mask=_mask(eng))
        sent += len(eng)

    when = []
    for s in range(S):
        for k, call in enumerate(_step3(topo, grp, red, s)):
            when += [(k, s, len(eng)) for dst, eng in call if dst == core]
    far = sorted(e for e in when if e[1] != i)
    own = [e for e in when if e[1] == i]
    plan = [(g.sync, sem.st0, [far[0], far[2]]), (g.scalar, sem.st1, [far[1], own[0]])]
    for q, done, todo in plan:
        for k, s, n in todo:
            q.wait_ge(sem["p3_%d" % s], n)
            q.dma_start(T.y[:, s * BL:(s + 1) * BL], T.yl[:, s * BL:(s + 1) * BL]).then_inc(done, 16)
        q.wait_ge(done, 16 * len(todo))
    g.wait_ge(sem.lsem, sent)


def _reducer(g, core, T, topo, groups, red):
    sem = T.sem
    owner = [c for c in red if red[c] == core][0]
    gi = [k for k in range(G) if owner in groups[k]][0]
    grp = groups[gi]
    s = grp.index(owner)
    V, add, mult = g.vector, AluOpType.add, AluOpType.mult
    nev = [0]

    def ev():
        nev[0] += 1
        return sem["e%d" % (nev[0] - 1)]

    V.memset(T.ones[:, :], 1.0).then_inc(sem.ms, 1)
    g.wait_ge(sem.ms, 1)
    g.affine_select(T.idn[:, :], T.ones[:, :], [[-1, 128]], AluOpType.is_equal, 0.0, 0, 1).then_inc(sem.idn, 1)

    off, spare = _engines(topo, core, owner, red[grp[(s + 1) % S]])
    cnt = [len(off)] * (S - 1) + [len(spare)]
    L = [T.l1[:, j * PS:j * PS + PW] for j in range(S)]
    h = len(off) // 2

    def step2(stage, src):
        trs = []
        for k in range(1, G):
            go = (gi + k) % G
            dst = red[groups[go][s]]
            slot = (gi - go - 1) % G
            rid, pid = topo.addr(dst, core)
            at = (2 * stage + slot) * PS
            trs.append(RemoteDMATransfer(dst_ids=[DstId(rid=rid, pnc=pid)], dma_engine_mask=_mask(off[(k - 1) * h:k * h]),
                                         remote_sem=sem["p2%s_%d" % ("ab"[stage], slot)], src=src,
                                         dst=T.l2[:, at:at + PW]))
        g.remote_dma_fused(trs, local_sem=sem.lsem)

    g.wait_ge(sem.p1_0, cnt[0])
    step2(0, L[0])
    pa, b0, b1, base = T.ps2[:, 0:PW], T.ps3[:, 0:PW], T.ps2[:, 256:256 + PW], T.ps3[:, 256:256 + PW]
    e_a, e_part, e_b0, e_b1, e_base = (ev() for _ in range(5))
    V.wait_ge(sem.p1_1, cnt[1])
    V.wait_ge(sem.p1_2, cnt[2])
    V.tensor_tensor(pa, L[1], L[2], add).then_inc(e_a, 1)
    V.wait_ge(sem.p1_3, cnt[3])
    V.wait_ge(e_a, 1)
    V.tensor_tensor(T.part[:, 0:PW], pa, L[3], add).then_inc(e_part, 1)
    g.wait_ge(e_part, 1)
    step2(1, T.part[:, 0:PW])
    sent = 4 * h
    V.wait_ge(sem.p1_0, cnt[0])
    V.wait_ge(e_part, 1)
    V.tensor_tensor(b0, T.part[:, 0:PW], L[0], add).then_inc(e_b0, 1)
    V.wait_ge(sem.p2a_0, h)
    V.wait_ge(e_b0, 1)
    V.tensor_tensor(b1, b0, T.l2[:, 0:PW], add).then_inc(e_b1, 1)
    V.wait_ge(sem.p2a_1, h)
    V.wait_ge(e_b1, 1)
    V.tensor_tensor(base, b1, T.l2[:, PS:PS + PW], add).then_inc(e_base, 1)

    A0, A1 = T.l2[:, 2 * PS:3 * PS], T.l2[:, 3 * PS:4 * PS]
    s1, s2, cw = T.st[:, 0:1], T.st[:, 1:2], T.st[:, 2:3]
    pt, pt2 = T.psc[:, 0:128], T.psc[:, 128:256]
    c_a, c_c, c_sd, c_nmu, c_r = (T.col[:, k:k + 1] for k in range(5))
    e1, e2, e3, e4, e5, e6, e7, e8 = (ev() for _ in range(8))
    V.wait_ge(e_base, 1)
    V.wait_ge(sem.p2b_0, h)
    V.tensor_tensor(T.sta[:, 0:3], base[:, 128:PW], A0[:, 128:PW], add).then_inc(e1, 1)
    V.wait_ge(sem.p2b_1, h)
    V.wait_ge(e1, 1)
    V.tensor_tensor(T.st[:, 0:3], T.sta[:, 0:3], A1[:, 128:PW], add).then_inc(e2, 1)
    V.wait_ge(e2, 1)
    V.tensor_scalar(c_a, s1, s1, -1.0 / D, mult, mult).then_inc(e3, 1)
    V.wait_ge(e3, 1)
    V.tensor_tensor(c_c, c_a, s2, add).then_inc(e4, 1)
    g.scalar.wait_ge(e4, 1)
    g.scalar.activation(c_sd, c_c, ActivationFunctionType.Sqrt, bias=EPS, scale=1.0 / D).then_inc(e5, 1)
    V.wait_ge(sem.idn, 1)
    V.tensor_scalar(T.dcw[:, :], T.idn[:, :], cw, None, mult).then_inc(e6, 1)
    g.tensor.wait_ge(sem.ms, 1)
    g.tensor.wait_ge(e6, 1)
    g.tensor.matmul(T.ps0[:, 0:128], T.ones[:, :], T.dcw[:, :], True, True).then_inc(e7, 1)
    V.tensor_scalar(c_nmu, s1, -1.0 / D, None, mult).then_inc(e8, 1)
    e9, e10, e11, e12, e13, e14, e15, e16 = (ev() for _ in range(8))
    V.tensor_tensor(pt, base[:, 0:128], A0[:, 0:128], add).then_inc(e9, 1)
    V.wait_ge(e9, 1)
    V.tensor_tensor(pt2, pt, A1[:, 0:128], add).then_inc(e10, 1)
    V.wait_ge(e7, 1)
    V.wait_ge(e8, 1)
    V.tensor_scalar(T.tmp[:, :], T.ps0[:, 0:128], c_nmu, None, mult).then_inc(e11, 1)
    V.wait_ge(e10, 1)
    V.wait_ge(e11, 1)
    V.tensor_tensor(T.am[:, :], T.tmp[:, :], pt2, add).then_inc(e12, 1)
    V.wait_ge(e5, 1)
    V.reciprocal(c_r, c_sd).then_inc(e13, 1)
    V.wait_ge(e13, 1)
    V.tensor_scalar(T.dg[:, :], T.idn[:, :], c_r, None, mult).then_inc(e14, 1)
    g.tensor.wait_ge(e12, 1)
    g.tensor.wait_ge(e14, 1)
    g.tensor.matmul(T.ps1[:, 0:128], T.am[:, :], T.dg[:, :], True, True).then_inc(e15, 1)
    V.wait_ge(e15, 1)
    V.tensor_copy(T.yo[:, :], T.ps1[:, 0:128]).then_inc(e16, 1)

    g.wait_ge(e16, 1)
    for call in _step3(topo, grp, red, s):
        trs = []
        for dst, eng in call:
            rid, pid = topo.addr(dst, core)
            trs.append(RemoteDMATransfer(dst_ids=[DstId(rid=rid, pnc=pid)], dma_engine_mask=_mask(eng),
                                         remote_sem=sem["p3_%d" % s], src=T.yo[:, :], dst=T.yl[:, s * BL:(s + 1) * BL]))
            sent += len(eng)
        g.remote_dma_fused(trs, local_sem=sem.lsem)
    g.wait_ge(sem.lsem, sent)


def rank_program(g, core, T, topo):
    groups, red = _plan(T, topo)
    if T.rank_of(core) is not None:
        _rank(g, core, T, topo, groups, red)
    elif core in red.values():
        _reducer(g, core, T, topo, groups, red)
